import numpy as np
import ml_dtypes


def mxq(x, axis, fmt="e4m3"):
    dtype, down = {"e4m3": (ml_dtypes.float8_e4m3fn, 7), "e5m2": (ml_dtypes.float8_e5m2, 14)}[fmt]
    v = np.moveaxis(np.asarray(x, np.float32).astype(ml_dtypes.bfloat16).astype(np.float64), axis, -1)
    blocks = v.reshape(v.shape[:-1] + (-1, 32))
    amax = np.abs(blocks).max(-1, keepdims=True)
    byte = np.maximum(np.where(amax > 0, np.frexp(amax)[1] - 1 + 127, 0) - down, 1)
    scale = np.exp2(byte - 127.0)
    codes = (blocks / scale).astype(np.float32).astype(dtype).astype(np.float64)
    return np.moveaxis((codes * scale).reshape(v.shape), -1, axis)


WIDE = False


def mx_kscale(k):
    if not WIDE:
        return np.ones(k)
    levels = np.array([10, -10, 5, -5, 0])
    if k % 512:
        return np.exp2(np.random.permutation(np.resize(levels, k // 32))).repeat(32)
    a = np.empty((k // 512, 16))
    for p in range(k // 512):
        a[p, :8] = np.random.permutation(np.resize(levels, 8))
        for g in range(8):
            far = levels[np.abs(levels - a[p, g]) >= 10]
            a[p, g + 8] = far[np.random.randint(len(far))]
    return np.exp2(a.ravel()).repeat(32)


BF16 = ml_dtypes.bfloat16


def bf(x):
    return np.asarray(x, np.float32).astype(BF16)


def f64(x):
    return np.asarray(x).astype(np.float64)


E2M1 = np.array([0.0, 0.5, 1.0, 1.5, 2.0, 3.0, 4.0, 6.0, -0.0, -0.5, -1.0, -1.5, -2.0, -3.0, -4.0, -6.0])


def pack_weight(w, fmt):
    k, n = w.shape
    w = f64(bf(w)).reshape(k // 32, 32, n)
    amax = np.abs(w).max(1)
    if fmt == "e4m3":
        byte = np.frexp(amax)[1] - 1 + 127 - 7
    else:
        mant, ex = np.frexp(amax / 6.0)
        byte = np.where(mant > 0.5, ex, ex - 1) + 127
    byte = np.clip(np.where(amax > 0, byte, 1), 1, 254)
    scaled = (w * np.exp2(127.0 - byte)[:, None, :]).reshape(k, n).astype(np.float32)
    by_word = np.ascontiguousarray(scaled.reshape(k // 512, 128, 4, n).transpose(0, 1, 3, 2))
    if fmt == "e4m3":
        words = by_word.astype(ml_dtypes.float8_e4m3fn).view(np.uint8)
    else:
        c = by_word.astype(ml_dtypes.float4_e2m1fn).view(np.uint8) & 0xF
        words = c[..., 0::2] | (c[..., 1::2] << 4)
    return np.ascontiguousarray(words), np.ascontiguousarray(byte.astype(np.uint8).reshape(k // 512, 16, n))


def unpack_weight(words, scales, fmt):
    g, p, n, _ = words.shape
    if fmt == "e4m3":
        vals = np.ascontiguousarray(words).view(ml_dtypes.float8_e4m3fn).astype(np.float64)
    else:
        nib = np.empty((g, p, n, 4), np.uint8)
        nib[..., 0::2] = words & 0xF
        nib[..., 1::2] = words >> 4
        vals = E2M1[nib]
    vals = vals * np.repeat(np.exp2(scales.astype(np.float64) - 127.0), 8, axis=1)[..., None]
    return vals.transpose(0, 1, 3, 2).reshape(g * 512, n)
def pack4(w):
    words, scales = pack_weight(w, "e2m1")
    return words.reshape(words.shape[0], 128, -1), scales


def unpack4(words, scales):
    return unpack_weight(words.reshape(words.shape[0], 128, -1, 2), scales, "e2m1")


M, K, D, N = 2048, 1024, 512, 1536


def setup_inputs():
    s = mx_kscale(K)
    r = mx_kscale(D)
    z = np.random.standard_normal((M, K)) * s
    A = 0.5 * np.random.standard_normal((K, N)) / np.sqrt(K) / s[:, None]
    a_words, a_scales = pack4(A)
    x = np.random.standard_normal((M, D)) * r
    B = 0.4 * np.random.standard_normal((D, N)) / np.sqrt(D) / r[:, None]
    return {"z": bf(z),
            "a_words": a_words,
            "a_scales": a_scales,
            "x": bf(x),
            "b": bf(B),
            "mu": bf(0.4 * np.random.standard_normal(N)),
            "dose": bf(np.exp(0.3 * np.random.standard_normal(M)))}


def reference(z, a_words, a_scales, x, b, mu, dose):
    random_part = mxq(f64(z), 1, "e4m3") @ unpack4(a_words, a_scales)
    covariate_part = mxq(f64(x), 1, "e4m3") @ mxq(f64(b), 0, "e4m3")
    log_conc = random_part + covariate_part + f64(mu)
    return f64(dose)[:, None] * np.exp(log_conc)

@@ -1,0 +1,352 @@
+from contextlib import ExitStack
+
+import concourse.mybir as mybir
+from concourse.masks import make_identity
+
+M, K, D, N = 2048, 1024, 512, 1536
+FLOPS = 2 * M * N * (K + D)
+
+F32 = mybir.dt.float32
+BF16 = mybir.dt.bfloat16
+I32 = mybir.dt.int32
+U32 = mybir.dt.uint32
+U8 = mybir.dt.uint8
+FP8X4 = mybir.dt.float8_e4m3fn_x4
+FP4X4 = mybir.dt.float4_e2m1fn_x4
+ACT = mybir.ActivationFunctionType
+ALU = mybir.AluOpType
+
+P = 128
+TILES = M // P
+PAIRS = TILES // 2
+W = 512
+THIRDS = N // W
+
+
+def tile_population_pk_elasticities_s1_kernel(tc, z, a_words, a_scales, x, b, mu, dose, out):
+    nc = tc.nc
+    z_rows = z.rearrange("(p i) k -> p i k", i=TILES)
+    x_rows = x.rearrange("(p i) k -> p i k", i=TILES)
+    out_rows = out.rearrange("(p i) n -> p i n", i=TILES)
+    b_rows = b.rearrange("(p j) n -> p j n", j=4)
+
+    with ExitStack() as ctx:
+        keep = ctx.enter_context(tc.tile_pool(name="keep", bufs=1))
+        raw = ctx.enter_context(tc.tile_pool(name="raw", bufs=6))
+        words_pool = ctx.enter_context(tc.tile_pool(name="words", bufs=3))
+        grouped_pool = ctx.enter_context(tc.tile_pool(name="grouped", bufs=4))
+        outs = ctx.enter_context(tc.tile_pool(name="outs", bufs=8))
+        turn_psum = ctx.enter_context(tc.psum_pool(name="turn", bufs=1))
+        acc_psum = ctx.enter_context(tc.psum_pool(name="acc", bufs=5))
+        ctx.enter_context(tc.manual_schedule())
+
+        z_raw, x_raw, turned, grouped = {}, {}, {}, {}
+        codes, scales = {}, {}
+        a_codes, b_raw, b_grouped, b_codes, b_scales = {}, {}, {}, {}, {}
+
+        def load_z(pair, half=None):
+            if pair not in z_raw:
+                z_tile = raw.tile([P, 2, K], BF16, tag="z_raw", name="z_raw")
+                z_raw[pair] = z_tile
+            i = slice(0, 2) if half is None else slice(half, half + 1)
+            r = slice(2 * pair + i.start, 2 * pair + i.stop)
+            nc.sync.dma_start(out=z_raw[pair][:, i, :], in_=z_rows[:, r, :])
+
+        def load_x(pair):
+            x_tile = raw.tile([P, 2, D], BF16, tag="x_raw", name="x_raw")
+            x_raw[pair] = x_tile
+            nc.sync.dma_start(out=x_tile[:], in_=x_rows[:, 2 * pair : 2 * pair + 2, :])
+
+        def load_a(third):
+            a_tile = keep.tile([P, 2, 2 * W], U8, tag="a%d" % third, name="a%d" % third, align_bytes=64)
+            a_codes[third] = a_tile
+            cols = slice(2 * W * third, 2 * W * (third + 1))
+            nc.sync.dma_start(out=a_tile[:].bitcast(I32), in_=a_words.rearrange("g p n -> p g n")[:, :, cols].bitcast(I32))
+
+        def load_b(third):
+            b_tile = keep.tile([P, 4, W], BF16, tag="b_raw%d" % third, name="b_raw%d" % third)
+            b_raw[third] = b_tile
+            nc.sync.dma_start(out=b_tile[:], in_=b_rows[:, :, W * third : W * (third + 1)])
+
+        def permute(pair, bank):
+            if bank == 2:
+                src = x_raw[pair][:].rearrange("p i k -> p (i k)")
+            else:
+                src = z_raw[pair][:, bank, :]
+            w_tile = words_pool.tile([P, 2, 256], F32, tag="w%d" % bank, name="w%d" % bank)
+            turned[pair, bank] = w_tile
+            nc.vector.tensor_copy(out=w_tile[:], in_=src.bitcast(F32).rearrange("p (w u) -> p u w", u=2))
+
+        def in_order(pair, bank):
+            if bank == 2:
+                src = x_raw[pair][:].rearrange("p i k -> p (i k)")
+            else:
+                src = z_raw[pair][:, bank, :]
+            turned[pair, bank] = src.bitcast(F32).rearrange("p (w u) -> p u w", u=2)
+
+        def turn(pair, bank, slot=None):
+            w_tile = turned[pair, bank]
+            slot = bank if slot is None else slot
+            ps = turn_psum.tile([P, 2, 2, P], F32, tag="turn%d" % slot, name="turn%d" % slot)
+            for k in range(2):
+                for u in range(2):
+                    nc.tensor.transpose(ps[:, k, u, :], w_tile[:, u, P * k : P * (k + 1)], ident[:])
+            turned[pair, bank] = ps
+
+        def empty(pair, bank, engine_copy=nc.scalar.copy):
+            g_tile = grouped_pool.tile([P, 1024], BF16, tag="grouped", name="grouped", align_bytes=64)
+            grouped[pair, bank] = g_tile
+            engine_copy(
+                out=g_tile[:].bitcast(F32).rearrange("p (k r u) -> p k r u", k=2, u=2),
+                in_=turned[pair, bank][:].rearrange("p k u r -> p k r u"),
+            )
+
+        def quantize(pair, bank):
+            c_tile = keep.tile([P, 256], U32, tag="c%d_%d" % (pair, bank), name="c%d_%d" % (pair, bank), align_bytes=64)
+            s_tile = keep.tile([P, 256], U8, tag="s%d_%d" % (pair, bank), name="s%d_%d" % (pair, bank), align_bytes=64)
+            codes[pair, bank], scales[pair, bank] = c_tile, s_tile
+            nc.vector.quantize_mx(out=c_tile[:].bitcast(FP8X4), scales=s_tile[:], in_=grouped[pair, bank][:])
+
+        def interleave_b(third, half, engine_copy):
+            if third not in b_grouped:
+                g_tile = keep.tile([P, W, 4], BF16, tag="b_grouped%d" % third, name="b_grouped%d" % third, align_bytes=64)
+                c_tile = keep.tile([P, W], U32, tag="b_codes%d" % third, name="b_codes%d" % third, align_bytes=64)
+                s_tile = keep.tile([P, W], U8, tag="b_scales%d" % third, name="b_scales%d" % third, align_bytes=64)
+                b_grouped[third], b_codes[third], b_scales[third] = g_tile, c_tile, s_tile
+            cols = slice(256 * half, 256 * (half + 1))
+            engine_copy(
+                out=b_grouped[third][:, cols, :].rearrange("p (c i) t -> p c t i", i=4),
+                in_=b_raw[third][:, :, cols].rearrange("p t (c i) -> p c t i", i=4),
+            )
+
+        def quantize_b(third, half):
+            cols = slice(256 * half, 256 * (half + 1))
+            nc.vector.quantize_mx(
+                out=b_codes[third][:, cols].bitcast(FP8X4),
+                scales=b_scales[third][:, cols],
+                in_=b_grouped[third][:, cols, :].rearrange("p n t -> p (n t)"),
+            )
+            b_done.add((third, half))
+
+        def z_pass(acc, pair, i, third, g):
+            nc.tensor.matmul_mx(
+                out=acc[:],
+                lhsT=codes[pair, i][:, P * g : P * (g + 1)].bitcast(FP8X4),
+                lhsT_scale=scales[pair, i][:, P * g : P * (g + 1)],
+                rhs=a_codes[third][:, g, :].bitcast(FP4X4),
+                rhs_scale=a_scale[:, g, W * third : W * (third + 1)],
+                start=(g == 0),
+                stop=False,
+            )
+
+        def x_pass(acc, pair, i, third):
+            nc.tensor.matmul_mx(
+                out=acc[:],
+                lhsT=codes[pair, 2][:, P * i : P * (i + 1)].bitcast(FP8X4),
+                lhsT_scale=scales[pair, 2][:, P * i : P * (i + 1)],
+                rhs=b_codes[third][:].bitcast(FP8X4),
+                rhs_scale=b_scales[third][:],
+                start=False,
+                stop=True,
+            )
+
+        def new_acc():
+            acc = acc_psum.tile([P, W], F32, tag="acc", name="acc")
+            return acc
+
+        out_tile = {}
+        b_done = set()
+
+        def add_mu(acc, pair, i, third):
+            if i == 0:
+                o_tile = outs.tile([P, 2, W], F32, tag="o", name="o")
+                out_tile[pair, third] = o_tile
+            nc.vector.tensor_tensor(out=out_tile[pair, third][:, i, :], in0=acc[:], in1=mu_all[:, W * third : W * (third + 1)], op=ALU.add)
+
+        def exponential(pair, i, third):
+            o = out_tile[pair, third][:, i, :]
+            nc.scalar.activation(out=o, in_=o, func=ACT.Exp, bias=log_dose[:, 2 * pair + i : 2 * pair + i + 1])
+
+        def store(pair, third):
+            nc.sync.dma_start(out=out_rows[:, 2 * pair : 2 * pair + 2, W * third : W * (third + 1)], in_=out_tile[pair, third][:])
+
+        ident = keep.tile([P, P], F32)
+        make_identity(nc, ident[:])
+        dose_raw = keep.tile([P, TILES], BF16)
+        mu_raw = keep.tile([P, 12], BF16)
+        nc.gpsimd.dma_start(out=mu_raw[:], in_=mu.rearrange("(p c) -> p c", c=12))
+        nc.gpsimd.dma_start(out=dose_raw[:], in_=dose.rearrange("(p i) -> p i", i=TILES))
+
+        a_scale = keep.tile([P, 2, N], U8, align_bytes=64)
+        nc.vector.memset(a_scale[:].rearrange("p g n -> p (g n)").bitcast(I32), 0)
+        one = keep.tile([P, 1], F32)
+        nc.vector.memset(one[:], 1.0)
+        warm = keep.tile([P, 1], F32)
+        nc.scalar.activation(out=warm[:], in_=one[:], func=ACT.Ln)
+
+        load_z(0, 0)
+        load_z(0, 1)
+        load_a(0)
+        load_z(1)
+        for q in range(4):
+            nc.sync.dma_start(
+                out=a_scale[32 * q : 32 * q + 4, :, :].bitcast(I32),
+                in_=a_scales[:, 4 * q : 4 * q + 4, :].rearrange("g r n -> r g n").bitcast(I32),
+            )
+        load_b(0)
+        load_x(0)
+        load_x(1)
+        load_a(1)
+        load_b(1)
+        load_z(2)
+        load_x(2)
+        load_a(2)
+        load_b(2)
+        load_z(3)
+        load_x(3)
+        load_z(4)
+        load_x(4)
+
+        ident_b = keep.tile([P, P], BF16)
+        nc.vector.tensor_copy(out=ident_b[:], in_=ident[:])
+        parts = keep.tile([P, 3, TILES], F32)
+        logs = keep.tile([P, 3, TILES], F32)
+        log_sum = keep.tile([P, TILES], F32)
+        log_dose = keep.tile([P, TILES], F32)
+        mu_all = keep.tile([P, N], BF16)
+        mu_cols = mu_all[:].rearrange("p (n c) -> p n c", c=12)
+
+        mu_banks = {}
+
+        def mu_columns(c0, cn, slot):
+            mu_ps = turn_psum.tile([P, cn, P], BF16, tag="turn%d" % slot, name="mu_ps")
+            for c in range(cn):
+                nc.tensor.transpose(mu_ps[:, c, :], mu_raw[:, c0 + c : c0 + c + 1].to_broadcast([P, P]), ident_b[:])
+            mu_banks[c0] = mu_ps
+
+        def mu_spread(c0, cn, engine_copy):
+            engine_copy(out=mu_cols[:, :, c0 : c0 + cn], in_=mu_banks[c0][:].rearrange("p c n -> p n c"))
+
+        def z_half(accs, pair):
+            for i in range(2):
+                for g in range(2):
+                    z_pass(accs[i], pair, i, 0, g)
+
+        V, S = nc.vector.tensor_copy, nc.scalar.copy
+        for i in range(2):
+            in_order(0, i)
+            turn(0, i)
+        mu_columns(0, 8, 2)
+        mu_acc = acc_psum.tile([P, 4, P], BF16, tag="acc", name="mu_acc")
+        for c in range(4):
+            nc.tensor.transpose(mu_acc[:, c, :], mu_raw[:, 8 + c : 9 + c].to_broadcast([P, P]), ident_b[:])
+        mu_banks[8] = mu_acc
+        for i in range(2):
+            empty(0, i)
+            quantize(0, i)
+        nc.vector.tensor_scalar(out=parts[:, 0, :], in0=dose_raw[:], scalar1=2.0**-63, op0=ALU.max, scalar2=2.0**64, op1=ALU.min)
+        nc.vector.tensor_scalar(out=parts[:, 1, :], in0=dose_raw[:], scalar1=2.0**63, op0=ALU.mult, scalar2=1.0, op1=ALU.min)
+        nc.vector.tensor_scalar(out=parts[:, 2, :], in0=dose_raw[:], scalar1=2.0**-64, op0=ALU.mult, scalar2=1.0, op1=ALU.max)
+        nc.scalar.activation(out=logs[:], in_=parts[:], func=ACT.Ln)
+        nc.scalar.activation(out=warm[:], in_=one[:], func=ACT.Exp)
+        acc0 = [new_acc(), new_acc()]
+        z_half(acc0, 0)
+        for i in range(2):
+            in_order(1, i)
+            turn(1, i)
+        mu_spread(0, 8, S)
+        interleave_b(0, 0, V)
+        interleave_b(0, 1, V)
+        quantize_b(0, 0)
+        in_order(0, 2)
+        turn(0, 2)
+        empty(1, 0, S)
+        empty(1, 1, V)
+        mu_spread(8, 4, S)
+        quantize(1, 0)
+        quantize(1, 1)
+        quantize_b(0, 1)
+        empty(0, 2)
+        acc1 = [new_acc(), new_acc()]
+        z_half(acc1, 1)
+        in_order(1, 2)
+        turn(1, 2, 0)
+        quantize(0, 2)
+        empty(1, 2)
+        for i in range(2):
+            x_pass(acc0[i], 0, i, 0)
+        interleave_b(1, 0, V)
+        interleave_b(1, 1, S)
+        quantize(1, 2)
+        nc.vector.tensor_tensor(out=log_sum[:], in0=logs[:, 0, :], in1=logs[:, 1, :], op=ALU.add)
+        add_mu(acc0[0], 0, 0, 0)
+        for i in range(2):
+            x_pass(acc1[i], 1, i, 0)
+        nc.vector.tensor_tensor(out=log_dose[:], in0=log_sum[:], in1=logs[:, 2, :], op=ALU.add)
+        add_mu(acc0[1], 0, 1, 0)
+        exponential(0, 0, 0)
+        exponential(0, 1, 0)
+        store(0, 0)
+        quantize_b(1, 0)
+        quantize_b(1, 1)
+        for bank in range(3):
+            in_order(2, bank)
+
+        add_mu(acc1[0], 1, 0, 0)
+        exponential(1, 0, 0)
+        add_mu(acc1[1], 1, 1, 0)
+        late = [(1, 1, 0)]
+
+        def late_exponential():
+            if late:
+                pair, i, third = late.pop(0)
+                exponential(pair, i, third)
+                if i == 1:
+                    store(pair, third)
+
+        def do_unit(pair, third, work):
+            for i in range(2):
+                acc = new_acc()
+                for g in range(2):
+                    z_pass(acc, pair, i, third, g)
+                x_pass(acc, pair, i, third)
+                for item in work[i]:
+                    item[0](*item[1:])
+                late_exponential()
+                add_mu(acc, pair, i, third)
+                late.append((pair, i, third))
+
+        def group(pair, units, extra=()):
+            nxt = pair + 1
+            has_next = nxt < PAIRS
+            if pair < PAIRS:
+                for bank in range(3):
+                    turn(pair, bank)
+                empty(pair, 0)
+                late_exponential()
+                empty(pair, 1)
+                empty(pair, 2)
+                if has_next:
+                    permute(nxt, 0)
+                    permute(nxt, 1)
+                    if nxt + 1 < PAIRS and nxt + 1 > 4:
+                        load_z(nxt + 1)
+                        load_x(nxt + 1)
+                quantize(pair, 0)
+            works = [[] for half in range(2 * len(units))]
+            if pair < PAIRS:
+                works[1].append((quantize, pair, 1))
+                works[2].append((quantize, pair, 2))
+                if has_next:
+                    works[3].append((permute, nxt, 2))
+            for k in range(len(extra)):
+                works[k] += extra[k]
+            for u in range(len(units)):
+                do_unit(units[u][0], units[u][1], works[2 * u : 2 * u + 2])
+
+        group(2, [(0, 1), (1, 1)], [[(interleave_b, 2, 0, V)], [], [(interleave_b, 2, 1, V)], []])
+        group(3, [(2, 0), (2, 1)], [[(quantize_b, 2, 0)], [(quantize_b, 2, 1)]])
+        for pair in range(3, PAIRS - 1):
+            group(pair + 1, [(pair, 0), (pair, 1), (pair - 3, 2)])
+        group(PAIRS, [(PAIRS - 1, 0), (PAIRS - 1, 1)] + [(pair, 2) for pair in range(PAIRS - 4, PAIRS)])
+        late_exponential()

@@ -21,6 +21,7 @@ TILES = M // P
 PAIRS = TILES // 2
 W = 512
 THIRDS = N // W
+FIRST_PERMUTED = 4
 
 
 def tile_population_pk_elasticities_s1_kernel(tc, z, a_words, a_scales, x, b, mu, dose, out):
@@ -32,7 +33,7 @@ def tile_population_pk_elasticities_s1_kernel(tc, z, a_words, a_scales, x, b, mu
 
     with ExitStack() as ctx:
         keep = ctx.enter_context(tc.tile_pool(name="keep", bufs=1))
-        raw = ctx.enter_context(tc.tile_pool(name="raw", bufs=6))
+        raw = ctx.enter_context(tc.tile_pool(name="raw", bufs=8))
         words_pool = ctx.enter_context(tc.tile_pool(name="words", bufs=3))
         grouped_pool = ctx.enter_context(tc.tile_pool(name="grouped", bufs=4))
         outs = ctx.enter_context(tc.tile_pool(name="outs", bufs=8))
@@ -57,10 +58,11 @@ def tile_population_pk_elasticities_s1_kernel(tc, z, a_words, a_scales, x, b, mu
             x_raw[pair] = x_tile
             nc.sync.dma_start(out=x_tile[:], in_=x_rows[:, 2 * pair : 2 * pair + 2, :])
 
-        def load_a(third):
-            a_tile = keep.tile([P, 2, 2 * W], U8, tag="a%d" % third, name="a%d" % third, align_bytes=64)
-            a_codes[third] = a_tile
-            cols = slice(2 * W * third, 2 * W * (third + 1))
+        def load_a(first, count):
+            a_tile = keep.tile([P, 2, 2 * W * count], U8, tag="a%d" % first, name="a%d" % first, align_bytes=64)
+            for third in range(first, first + count):
+                a_codes[third] = a_tile[:, :, 2 * W * (third - first) : 2 * W * (third - first + 1)]
+            cols = slice(2 * W * first, 2 * W * (first + count))
             nc.sync.dma_start(out=a_tile[:].bitcast(I32), in_=a_words.rearrange("g p n -> p g n")[:, :, cols].bitcast(I32))
 
         def load_b(third):
@@ -157,56 +159,56 @@ def tile_population_pk_elasticities_s1_kernel(tc, z, a_words, a_scales, x, b, mu
         out_tile = {}
         b_done = set()
 
-        def add_mu(acc, pair, i, third):
-            if i == 0:
+        def add_mu(acc, pair, i, third, cols=slice(0, W)):
+            if (pair, third) not in out_tile:
                 o_tile = outs.tile([P, 2, W], F32, tag="o", name="o")
                 out_tile[pair, third] = o_tile
-            nc.vector.tensor_tensor(out=out_tile[pair, third][:, i, :], in0=acc[:], in1=mu_all[:, W * third : W * (third + 1)], op=ALU.add)
+            mu_part = mu_all[:, W * third + cols.start : W * third + cols.stop]
+            nc.vector.tensor_tensor(out=out_tile[pair, third][:, i, cols], in0=acc[:, cols], in1=mu_part, op=ALU.add)
 
-        def exponential(pair, i, third):
-            o = out_tile[pair, third][:, i, :]
+        def exponential(pair, i, third, cols=slice(0, W)):
+            o = out_tile[pair, third][:, i, cols]
             nc.scalar.activation(out=o, in_=o, func=ACT.Exp, bias=log_dose[:, 2 * pair + i : 2 * pair + i + 1])
 
-        def store(pair, third):
-            nc.sync.dma_start(out=out_rows[:, 2 * pair : 2 * pair + 2, W * third : W * (third + 1)], in_=out_tile[pair, third][:])
+        def store(pair, third, i=slice(0, 2), cols=slice(0, W)):
+            rows = slice(2 * pair + i.start, 2 * pair + i.stop)
+            out_cols = slice(W * third + cols.start, W * third + cols.stop)
+            nc.sync.dma_start(out=out_rows[:, rows, out_cols], in_=out_tile[pair, third][:, i, cols])
 
-        ident = keep.tile([P, P], F32)
-        make_identity(nc, ident[:])
         dose_raw = keep.tile([P, TILES], BF16)
         mu_raw = keep.tile([P, 12], BF16)
-        nc.gpsimd.dma_start(out=mu_raw[:], in_=mu.rearrange("(p c) -> p c", c=12))
-        nc.gpsimd.dma_start(out=dose_raw[:], in_=dose.rearrange("(p i) -> p i", i=TILES))
+        ident = keep.tile([P, P], F32)
+        make_identity(nc, ident[:])
+        nc.scalar.dma_start(out=mu_raw[:], in_=mu.rearrange("(p c) -> p c", c=12))
+        nc.scalar.dma_start(out=dose_raw[:], in_=dose.rearrange("(p i) -> p i", i=TILES))
 
-        a_scale = keep.tile([P, 2, N], U8, align_bytes=64)
-        nc.vector.memset(a_scale[:].rearrange("p g n -> p (g n)").bitcast(I32), 0)
         one = keep.tile([P, 1], F32)
         nc.vector.memset(one[:], 1.0)
-        warm = keep.tile([P, 1], F32)
-        nc.scalar.activation(out=warm[:], in_=one[:], func=ACT.Ln)
-
+        a_scale = keep.tile([P, 2, N], U8, align_bytes=64)
+        nc.vector.memset(a_scale[:].rearrange("p g n -> p (g n)").bitcast(I32), 0)
         load_z(0, 0)
         load_z(0, 1)
-        load_a(0)
-        load_z(1)
         for q in range(4):
-            nc.sync.dma_start(
+            (nc.scalar if q < 3 else nc.gpsimd).dma_start(
                 out=a_scale[32 * q : 32 * q + 4, :, :].bitcast(I32),
                 in_=a_scales[:, 4 * q : 4 * q + 4, :].rearrange("g r n -> r g n").bitcast(I32),
             )
+        load_a(0, 2)
+        load_z(1)
         load_b(0)
         load_x(0)
         load_x(1)
-        load_a(1)
         load_b(1)
         load_z(2)
         load_x(2)
-        load_a(2)
+        load_a(2, 1)
         load_b(2)
-        load_z(3)
-        load_x(3)
-        load_z(4)
-        load_x(4)
+        for pair in range(3, 6):
+            load_z(pair)
+            load_x(pair)
 
+        warm = keep.tile([P, 1], F32)
+        nc.scalar.activation(out=warm[:], in_=one[:], func=ACT.Ln)
         ident_b = keep.tile([P, P], BF16)
         nc.vector.tensor_copy(out=ident_b[:], in_=ident[:])
         parts = keep.tile([P, 3, TILES], F32)
@@ -215,11 +217,10 @@ def tile_population_pk_elasticities_s1_kernel(tc, z, a_words, a_scales, x, b, mu
         log_dose = keep.tile([P, TILES], F32)
         mu_all = keep.tile([P, N], BF16)
         mu_cols = mu_all[:].rearrange("p (n c) -> p n c", c=12)
-
         mu_banks = {}
 
-        def mu_columns(c0, cn, slot):
-            mu_ps = turn_psum.tile([P, cn, P], BF16, tag="turn%d" % slot, name="mu_ps")
+        def mu_columns(c0, cn, pool, tag):
+            mu_ps = pool.tile([P, cn, P], BF16, tag=tag, name="mu_ps")
             for c in range(cn):
                 nc.tensor.transpose(mu_ps[:, c, :], mu_raw[:, c0 + c : c0 + c + 1].to_broadcast([P, P]), ident_b[:])
             mu_banks[c0] = mu_ps
@@ -236,59 +237,57 @@ def tile_population_pk_elasticities_s1_kernel(tc, z, a_words, a_scales, x, b, mu
         for i in range(2):
             in_order(0, i)
             turn(0, i)
-        mu_columns(0, 8, 2)
-        mu_acc = acc_psum.tile([P, 4, P], BF16, tag="acc", name="mu_acc")
-        for c in range(4):
-            nc.tensor.transpose(mu_acc[:, c, :], mu_raw[:, 8 + c : 9 + c].to_broadcast([P, P]), ident_b[:])
-        mu_banks[8] = mu_acc
-        for i in range(2):
-            empty(0, i)
-            quantize(0, i)
+        mu_columns(0, 8, turn_psum, "turn2")
+        mu_columns(8, 4, acc_psum, "acc")
         nc.vector.tensor_scalar(out=parts[:, 0, :], in0=dose_raw[:], scalar1=2.0**-63, op0=ALU.max, scalar2=2.0**64, op1=ALU.min)
         nc.vector.tensor_scalar(out=parts[:, 1, :], in0=dose_raw[:], scalar1=2.0**63, op0=ALU.mult, scalar2=1.0, op1=ALU.min)
         nc.vector.tensor_scalar(out=parts[:, 2, :], in0=dose_raw[:], scalar1=2.0**-64, op0=ALU.mult, scalar2=1.0, op1=ALU.max)
         nc.scalar.activation(out=logs[:], in_=parts[:], func=ACT.Ln)
         nc.scalar.activation(out=warm[:], in_=one[:], func=ACT.Exp)
-        acc0 = [new_acc(), new_acc()]
-        z_half(acc0, 0)
+        empty(0, 0, V)
+        empty(0, 1, V)
+        quantize(0, 0)
+        quantize(0, 1)
+        nc.vector.tensor_tensor(out=log_sum[:], in0=logs[:, 0, :], in1=logs[:, 1, :], op=ALU.add)
+        mu_spread(0, 8, S)
+        mu_spread(8, 4, S)
+        nc.vector.tensor_tensor(out=log_dose[:], in0=log_sum[:], in1=logs[:, 2, :], op=ALU.add)
         for i in range(2):
             in_order(1, i)
             turn(1, i)
-        mu_spread(0, 8, S)
-        interleave_b(0, 0, V)
-        interleave_b(0, 1, V)
-        quantize_b(0, 0)
+        acc0 = [new_acc(), new_acc()]
+        z_half(acc0, 0)
+        empty(1, 0)
+        empty(1, 1)
         in_order(0, 2)
-        turn(0, 2)
-        empty(1, 0, S)
-        empty(1, 1, V)
-        mu_spread(8, 4, S)
-        quantize(1, 0)
-        quantize(1, 1)
-        quantize_b(0, 1)
-        empty(0, 2)
-        acc1 = [new_acc(), new_acc()]
-        z_half(acc1, 1)
+        turn(0, 2, 2)
         in_order(1, 2)
         turn(1, 2, 0)
-        quantize(0, 2)
+        interleave_b(0, 0, V)
+        interleave_b(0, 1, V)
+        quantize(1, 0)
+        quantize(1, 1)
+        quantize_b(0, 0)
+        quantize_b(0, 1)
+        empty(0, 2)
         empty(1, 2)
+        acc1 = [new_acc(), new_acc()]
+        z_half(acc1, 1)
+        quantize(0, 2)
+        interleave_b(1, 1, S)
         for i in range(2):
             x_pass(acc0[i], 0, i, 0)
-        interleave_b(1, 0, V)
-        interleave_b(1, 1, S)
         quantize(1, 2)
-        nc.vector.tensor_tensor(out=log_sum[:], in0=logs[:, 0, :], in1=logs[:, 1, :], op=ALU.add)
+        interleave_b(1, 0, V)
         add_mu(acc0[0], 0, 0, 0)
         for i in range(2):
             x_pass(acc1[i], 1, i, 0)
-        nc.vector.tensor_tensor(out=log_dose[:], in0=log_sum[:], in1=logs[:, 2, :], op=ALU.add)
         add_mu(acc0[1], 0, 1, 0)
         exponential(0, 0, 0)
-        exponential(0, 1, 0)
-        store(0, 0)
         quantize_b(1, 0)
         quantize_b(1, 1)
+        exponential(0, 1, 0)
+        store(0, 0)
         for bank in range(3):
             in_order(2, bank)
 
@@ -327,18 +326,22 @@ def tile_population_pk_elasticities_s1_kernel(tc, z, a_words, a_scales, x, b, mu
                 empty(pair, 1)
                 empty(pair, 2)
                 if has_next:
-                    permute(nxt, 0)
-                    permute(nxt, 1)
-                    if nxt + 1 < PAIRS and nxt + 1 > 4:
-                        load_z(nxt + 1)
-                        load_x(nxt + 1)
+                    if nxt < FIRST_PERMUTED:
+                        for bank in range(3):
+                            in_order(nxt, bank)
+                    else:
+                        permute(nxt, 0)
+                        permute(nxt, 1)
+                    if nxt + 3 > 5 and nxt + 3 < PAIRS:
+                        load_z(nxt + 3)
+                        load_x(nxt + 3)
                 quantize(pair, 0)
             works = [[] for half in range(2 * len(units))]
             if pair < PAIRS:
                 works[1].append((quantize, pair, 1))
                 works[2].append((quantize, pair, 2))
-                if has_next:
-                    works[3].append((permute, nxt, 2))
+                if has_next and nxt >= FIRST_PERMUTED:
+                    works[0].append((permute, nxt, 2))
             for k in range(len(extra)):
                 works[k] += extra[k]
             for u in range(len(units)):
@@ -348,5 +351,21 @@ def tile_population_pk_elasticities_s1_kernel(tc, z, a_words, a_scales, x, b, mu
         group(3, [(2, 0), (2, 1)], [[(quantize_b, 2, 0)], [(quantize_b, 2, 1)]])
         for pair in range(3, PAIRS - 1):
             group(pair + 1, [(pair, 0), (pair, 1), (pair - 3, 2)])
-        group(PAIRS, [(PAIRS - 1, 0), (PAIRS - 1, 1)] + [(pair, 2) for pair in range(PAIRS - 4, PAIRS)])
-        late_exponential()
+        group(PAIRS, [(PAIRS - 1, 0), (PAIRS - 1, 1)] + [(pair, 2) for pair in range(PAIRS - 4, PAIRS - 1)])
+
+        last = PAIRS - 1
+        for i in range(2):
+            acc = new_acc()
+            for g in range(2):
+                z_pass(acc, last, i, 2, g)
+            x_pass(acc, last, i, 2)
+            late_exponential()
+            if i == 0:
+                add_mu(acc, last, 0, 2)
+                exponential(last, 0, 2)
+                store(last, 2, slice(0, 1))
+            else:
+                for cols in (slice(0, W // 2), slice(W // 2, W)):
+                    add_mu(acc, last, 1, 2, cols)
+                    exponential(last, 1, 2, cols)
+                    store(last, 2, slice(1, 2), cols)

from contextlib import ExitStack

import concourse.mybir as mybir
from concourse.masks import make_identity

M, K, D, N = 2048, 1024, 512, 1536
FLOPS = 2 * M * N * (K + D)

F32 = mybir.dt.float32
BF16 = mybir.dt.bfloat16
I32 = mybir.dt.int32
U32 = mybir.dt.uint32
U8 = mybir.dt.uint8
FP8X4 = mybir.dt.float8_e4m3fn_x4
FP4X4 = mybir.dt.float4_e2m1fn_x4
ACT = mybir.ActivationFunctionType
ALU = mybir.AluOpType

P = 128
TILES = M // P
PAIRS = TILES // 2
W = 512
THIRDS = N // W
FIRST_PERMUTED = 4


def tile_population_pk_elasticities_s1_kernel(tc, z, a_words, a_scales, x, b, mu, dose, out):
    nc = tc.nc
    z_rows = z.rearrange("(p i) k -> p i k", i=TILES)
    x_rows = x.rearrange("(p i) k -> p i k", i=TILES)
    out_rows = out.rearrange("(p i) n -> p i n", i=TILES)
    b_rows = b.rearrange("(p j) n -> p j n", j=4)

    with ExitStack() as ctx:
        keep = ctx.enter_context(tc.tile_pool(name="keep", bufs=1))
        raw = ctx.enter_context(tc.tile_pool(name="raw", bufs=8))
        words_pool = ctx.enter_context(tc.tile_pool(name="words", bufs=3))
        grouped_pool = ctx.enter_context(tc.tile_pool(name="grouped", bufs=4))
        outs = ctx.enter_context(tc.tile_pool(name="outs", bufs=8))
        turn_psum = ctx.enter_context(tc.psum_pool(name="turn", bufs=1))
        acc_psum = ctx.enter_context(tc.psum_pool(name="acc", bufs=5))
        ctx.enter_context(tc.manual_schedule())

        z_raw, x_raw, turned, grouped = {}, {}, {}, {}
        codes, scales = {}, {}
        a_codes, b_raw, b_grouped, b_codes, b_scales = {}, {}, {}, {}, {}

        def load_z(pair, half=None):
            if pair not in z_raw:
                z_tile = raw.tile([P, 2, K], BF16, tag="z_raw", name="z_raw")
                z_raw[pair] = z_tile
            i = slice(0, 2) if half is None else slice(half, half + 1)
            r = slice(2 * pair + i.start, 2 * pair + i.stop)
            nc.sync.dma_start(out=z_raw[pair][:, i, :], in_=z_rows[:, r, :])

        def load_x(pair):
            x_tile = raw.tile([P, 2, D], BF16, tag="x_raw", name="x_raw")
            x_raw[pair] = x_tile
            nc.sync.dma_start(out=x_tile[:], in_=x_rows[:, 2 * pair : 2 * pair + 2, :])

        def load_a(first, count):
            a_tile = keep.tile([P, 2, 2 * W * count], U8, tag="a%d" % first, name="a%d" % first, align_bytes=64)
            for third in range(first, first + count):
                a_codes[third] = a_tile[:, :, 2 * W * (third - first) : 2 * W * (third - first + 1)]
            cols = slice(2 * W * first, 2 * W * (first + count))
            nc.sync.dma_start(out=a_tile[:].bitcast(I32), in_=a_words.rearrange("g p n -> p g n")[:, :, cols].bitcast(I32))

        def load_b(third):
            b_tile = keep.tile([P, 4, W], BF16, tag="b_raw%d" % third, name="b_raw%d" % third)
            b_raw[third] = b_tile
            nc.sync.dma_start(out=b_tile[:], in_=b_rows[:, :, W * third : W * (third + 1)])

        def permute(pair, bank):
            if bank == 2:
                src = x_raw[pair][:].rearrange("p i k -> p (i k)")
            else:
                src = z_raw[pair][:, bank, :]
            w_tile = words_pool.tile([P, 2, 256], F32, tag="w%d" % bank, name="w%d" % bank)
            turned[pair, bank] = w_tile
            nc.vector.tensor_copy(out=w_tile[:], in_=src.bitcast(F32).rearrange("p (w u) -> p u w", u=2))

        def in_order(pair, bank):
            if bank == 2:
                src = x_raw[pair][:].rearrange("p i k -> p (i k)")
            else:
                src = z_raw[pair][:, bank, :]
            turned[pair, bank] = src.bitcast(F32).rearrange("p (w u) -> p u w", u=2)

        def turn(pair, bank, slot=None):
            w_tile = turned[pair, bank]
            slot = bank if slot is None else slot
            ps = turn_psum.tile([P, 2, 2, P], F32, tag="turn%d" % slot, name="turn%d" % slot)
            for k in range(2):
                for u in range(2):
                    nc.tensor.transpose(ps[:, k, u, :], w_tile[:, u, P * k : P * (k + 1)], ident[:])
            turned[pair, bank] = ps

        def empty(pair, bank, engine_copy=nc.scalar.copy):
            g_tile = grouped_pool.tile([P, 1024], BF16, tag="grouped", name="grouped", align_bytes=64)
            grouped[pair, bank] = g_tile
            engine_copy(
                out=g_tile[:].bitcast(F32).rearrange("p (k r u) -> p k r u", k=2, u=2),
                in_=turned[pair, bank][:].rearrange("p k u r -> p k r u"),
            )

        def quantize(pair, bank):
            c_tile = keep.tile([P, 256], U32, tag="c%d_%d" % (pair, bank), name="c%d_%d" % (pair, bank), align_bytes=64)
            s_tile = keep.tile([P, 256], U8, tag="s%d_%d" % (pair, bank), name="s%d_%d" % (pair, bank), align_bytes=64)
            codes[pair, bank], scales[pair, bank] = c_tile, s_tile
            nc.vector.quantize_mx(out=c_tile[:].bitcast(FP8X4), scales=s_tile[:], in_=grouped[pair, bank][:])

        def interleave_b(third, half, engine_copy):
            if third not in b_grouped:
                g_tile = keep.tile([P, W, 4], BF16, tag="b_grouped%d" % third, name="b_grouped%d" % third, align_bytes=64)
                c_tile = keep.tile([P, W], U32, tag="b_codes%d" % third, name="b_codes%d" % third, align_bytes=64)
                s_tile = keep.tile([P, W], U8, tag="b_scales%d" % third, name="b_scales%d" % third, align_bytes=64)
                b_grouped[third], b_codes[third], b_scales[third] = g_tile, c_tile, s_tile
            cols = slice(256 * half, 256 * (half + 1))
            engine_copy(
                out=b_grouped[third][:, cols, :].rearrange("p (c i) t -> p c t i", i=4),
                in_=b_raw[third][:, :, cols].rearrange("p t (c i) -> p c t i", i=4),
            )

        def quantize_b(third, half):
            cols = slice(256 * half, 256 * (half + 1))
            nc.vector.quantize_mx(
                out=b_codes[third][:, cols].bitcast(FP8X4),
                scales=b_scales[third][:, cols],
                in_=b_grouped[third][:, cols, :].rearrange("p n t -> p (n t)"),
            )
            b_done.add((third, half))

        def z_pass(acc, pair, i, third, g):
            nc.tensor.matmul_mx(
                out=acc[:],
                lhsT=codes[pair, i][:, P * g : P * (g + 1)].bitcast(FP8X4),
                lhsT_scale=scales[pair, i][:, P * g : P * (g + 1)],
                rhs=a_codes[third][:, g, :].bitcast(FP4X4),
                rhs_scale=a_scale[:, g, W * third : W * (third + 1)],
                start=(g == 0),
                stop=False,
            )

        def x_pass(acc, pair, i, third):
            nc.tensor.matmul_mx(
                out=acc[:],
                lhsT=codes[pair, 2][:, P * i : P * (i + 1)].bitcast(FP8X4),
                lhsT_scale=scales[pair, 2][:, P * i : P * (i + 1)],
                rhs=b_codes[third][:].bitcast(FP8X4),
                rhs_scale=b_scales[third][:],
                start=False,
                stop=True,
            )

        def new_acc():
            acc = acc_psum.tile([P, W], F32, tag="acc", name="acc")
            return acc

        out_tile = {}
        b_done = set()

        def add_mu(acc, pair, i, third, cols=slice(0, W)):
            if (pair, third) not in out_tile:
                o_tile = outs.tile([P, 2, W], F32, tag="o", name="o")
                out_tile[pair, third] = o_tile
            mu_part = mu_all[:, W * third + cols.start : W * third + cols.stop]
            nc.vector.tensor_tensor(out=out_tile[pair, third][:, i, cols], in0=acc[:, cols], in1=mu_part, op=ALU.add)

        def exponential(pair, i, third, cols=slice(0, W)):
            o = out_tile[pair, third][:, i, cols]
            nc.scalar.activation(out=o, in_=o, func=ACT.Exp, bias=log_dose[:, 2 * pair + i : 2 * pair + i + 1])

        def store(pair, third, i=slice(0, 2), cols=slice(0, W)):
            rows = slice(2 * pair + i.start, 2 * pair + i.stop)
            out_cols = slice(W * third + cols.start, W * third + cols.stop)
            nc.sync.dma_start(out=out_rows[:, rows, out_cols], in_=out_tile[pair, third][:, i, cols])

        dose_raw = keep.tile([P, TILES], BF16)
        mu_raw = keep.tile([P, 12], BF16)
        ident = keep.tile([P, P], F32)
        make_identity(nc, ident[:])
        nc.scalar.dma_start(out=mu_raw[:], in_=mu.rearrange("(p c) -> p c", c=12))
        nc.scalar.dma_start(out=dose_raw[:], in_=dose.rearrange("(p i) -> p i", i=TILES))

        one = keep.tile([P, 1], F32)
        nc.vector.memset(one[:], 1.0)
        a_scale = keep.tile([P, 2, N], U8, align_bytes=64)
        nc.vector.memset(a_scale[:].rearrange("p g n -> p (g n)").bitcast(I32), 0)
        load_z(0, 0)
        load_z(0, 1)
        for q in range(4):
            (nc.scalar if q < 3 else nc.gpsimd).dma_start(
                out=a_scale[32 * q : 32 * q + 4, :, :].bitcast(I32),
                in_=a_scales[:, 4 * q : 4 * q + 4, :].rearrange("g r n -> r g n").bitcast(I32),
            )
        load_a(0, 2)
        load_z(1)
        load_b(0)
        load_x(0)
        load_x(1)
        load_b(1)
        load_z(2)
        load_x(2)
        load_a(2, 1)
        load_b(2)
        for pair in range(3, 6):
            load_z(pair)
            load_x(pair)

        warm = keep.tile([P, 1], F32)
        nc.scalar.activation(out=warm[:], in_=one[:], func=ACT.Ln)
        ident_b = keep.tile([P, P], BF16)
        nc.vector.tensor_copy(out=ident_b[:], in_=ident[:])
        parts = keep.tile([P, 3, TILES], F32)
        logs = keep.tile([P, 3, TILES], F32)
        log_sum = keep.tile([P, TILES], F32)
        log_dose = keep.tile([P, TILES], F32)
        mu_all = keep.tile([P, N], BF16)
        mu_cols = mu_all[:].rearrange("p (n c) -> p n c", c=12)
        mu_banks = {}

        def mu_columns(c0, cn, pool, tag):
            mu_ps = pool.tile([P, cn, P], BF16, tag=tag, name="mu_ps")
            for c in range(cn):
                nc.tensor.transpose(mu_ps[:, c, :], mu_raw[:, c0 + c : c0 + c + 1].to_broadcast([P, P]), ident_b[:])
            mu_banks[c0] = mu_ps

        def mu_spread(c0, cn, engine_copy):
            engine_copy(out=mu_cols[:, :, c0 : c0 + cn], in_=mu_banks[c0][:].rearrange("p c n -> p n c"))

        def z_half(accs, pair):
            for i in range(2):
                for g in range(2):
                    z_pass(accs[i], pair, i, 0, g)

        V, S = nc.vector.tensor_copy, nc.scalar.copy
        for i in range(2):
            in_order(0, i)
            turn(0, i)
        mu_columns(0, 8, turn_psum, "turn2")
        mu_columns(8, 4, acc_psum, "acc")
        nc.vector.tensor_scalar(out=parts[:, 0, :], in0=dose_raw[:], scalar1=2.0**-63, op0=ALU.max, scalar2=2.0**64, op1=ALU.min)
        nc.vector.tensor_scalar(out=parts[:, 1, :], in0=dose_raw[:], scalar1=2.0**63, op0=ALU.mult, scalar2=1.0, op1=ALU.min)
        nc.vector.tensor_scalar(out=parts[:, 2, :], in0=dose_raw[:], scalar1=2.0**-64, op0=ALU.mult, scalar2=1.0, op1=ALU.max)
        nc.scalar.activation(out=logs[:], in_=parts[:], func=ACT.Ln)
        nc.scalar.activation(out=warm[:], in_=one[:], func=ACT.Exp)
        empty(0, 0, V)
        empty(0, 1, V)
        quantize(0, 0)
        quantize(0, 1)
        nc.vector.tensor_tensor(out=log_sum[:], in0=logs[:, 0, :], in1=logs[:, 1, :], op=ALU.add)
        mu_spread(0, 8, S)
        mu_spread(8, 4, S)
        nc.vector.tensor_tensor(out=log_dose[:], in0=log_sum[:], in1=logs[:, 2, :], op=ALU.add)
        for i in range(2):
            in_order(1, i)
            turn(1, i)
        acc0 = [new_acc(), new_acc()]
        z_half(acc0, 0)
        empty(1, 0)
        empty(1, 1)
        in_order(0, 2)
        turn(0, 2, 2)
        in_order(1, 2)
        turn(1, 2, 0)
        interleave_b(0, 0, V)
        interleave_b(0, 1, V)
        quantize(1, 0)
        quantize(1, 1)
        quantize_b(0, 0)
        quantize_b(0, 1)
        empty(0, 2)
        empty(1, 2)
        acc1 = [new_acc(), new_acc()]
        z_half(acc1, 1)
        quantize(0, 2)
        interleave_b(1, 1, S)
        for i in range(2):
            x_pass(acc0[i], 0, i, 0)
        quantize(1, 2)
        interleave_b(1, 0, V)
        add_mu(acc0[0], 0, 0, 0)
        for i in range(2):
            x_pass(acc1[i], 1, i, 0)
        add_mu(acc0[1], 0, 1, 0)
        exponential(0, 0, 0)
        quantize_b(1, 0)
        quantize_b(1, 1)
        exponential(0, 1, 0)
        store(0, 0)
        for bank in range(3):
            in_order(2, bank)

        add_mu(acc1[0], 1, 0, 0)
        exponential(1, 0, 0)
        add_mu(acc1[1], 1, 1, 0)
        late = [(1, 1, 0)]

        def late_exponential():
            if late:
                pair, i, third = late.pop(0)
                exponential(pair, i, third)
                if i == 1:
                    store(pair, third)

        def do_unit(pair, third, work):
            for i in range(2):
                acc = new_acc()
                for g in range(2):
                    z_pass(acc, pair, i, third, g)
                x_pass(acc, pair, i, third)
                for item in work[i]:
                    item[0](*item[1:])
                late_exponential()
                add_mu(acc, pair, i, third)
                late.append((pair, i, third))

        def group(pair, units, extra=()):
            nxt = pair + 1
            has_next = nxt < PAIRS
            if pair < PAIRS:
                for bank in range(3):
                    turn(pair, bank)
                empty(pair, 0)
                late_exponential()
                empty(pair, 1)
                empty(pair, 2)
                if has_next:
                    if nxt < FIRST_PERMUTED:
                        for bank in range(3):
                            in_order(nxt, bank)
                    else:
                        permute(nxt, 0)
                        permute(nxt, 1)
                    if nxt + 3 > 5 and nxt + 3 < PAIRS:
                        load_z(nxt + 3)
                        load_x(nxt + 3)
                quantize(pair, 0)
            works = [[] for half in range(2 * len(units))]
            if pair < PAIRS:
                works[1].append((quantize, pair, 1))
                works[2].append((quantize, pair, 2))
                if has_next and nxt >= FIRST_PERMUTED:
                    works[0].append((permute, nxt, 2))
            for k in range(len(extra)):
                works[k] += extra[k]
            for u in range(len(units)):
                do_unit(units[u][0], units[u][1], works[2 * u : 2 * u + 2])

        group(2, [(0, 1), (1, 1)], [[(interleave_b, 2, 0, V)], [], [(interleave_b, 2, 1, V)], []])
        group(3, [(2, 0), (2, 1)], [[(quantize_b, 2, 0)], [(quantize_b, 2, 1)]])
        for pair in range(3, PAIRS - 1):
            group(pair + 1, [(pair, 0), (pair, 1), (pair - 3, 2)])
        group(PAIRS, [(PAIRS - 1, 0), (PAIRS - 1, 1)] + [(pair, 2) for pair in range(PAIRS - 4, PAIRS - 1)])

        last = PAIRS - 1
        for i in range(2):
            acc = new_acc()
            for g in range(2):
                z_pass(acc, last, i, 2, g)
            x_pass(acc, last, i, 2)
            late_exponential()
            if i == 0:
                add_mu(acc, last, 0, 2)
                exponential(last, 0, 2)
                store(last, 2, slice(0, 1))
            else:
                for cols in (slice(0, W // 2), slice(W // 2, W)):
                    add_mu(acc, last, 1, 2, cols)
                    exponential(last, 1, 2, cols)
                    store(last, 2, slice(1, 2), cols)
